import numpy as np
import ml_dtypes


def mxq(x, axis, fmt="e4m3"):
    dtype, down = {"e4m3": (ml_dtypes.float8_e4m3fn, 7), "e5m2": (ml_dtypes.float8_e5m2, 14)}[fmt]
    v = np.moveaxis(np.asarray(x, np.float32).astype(ml_dtypes.bfloat16).astype(np.float64), axis, -1)
    blocks = v.reshape(v.shape[:-1] + (-1, 32))
    amax = np.abs(blocks).max(-1, keepdims=True)
    byte = np.maximum(np.where(amax > 0, np.frexp(amax)[1] - 1 + 127, 0) - down, 1)
    scale = np.exp2(byte - 127.0)
    codes = (blocks / scale).astype(np.float32).astype(dtype).astype(np.float64)
    return np.moveaxis((codes * scale).reshape(v.shape), -1, axis)


WIDE = False


def mx_kscale(k):
    if not WIDE:
        return np.ones(k)
    levels = np.array([10, -10, 5, -5, 0])
    if k % 512:
        return np.exp2(np.random.permutation(np.resize(levels, k // 32))).repeat(32)
    a = np.empty((k // 512, 16))
    for p in range(k // 512):
        a[p, :8] = np.random.permutation(np.resize(levels, 8))
        for g in range(8):
            far = levels[np.abs(levels - a[p, g]) >= 10]
            a[p, g + 8] = far[np.random.randint(len(far))]
    return np.exp2(a.ravel()).repeat(32)


BF16 = ml_dtypes.bfloat16


def bf(x):
    return np.asarray(x, np.float32).astype(BF16)


def f64(x):
    return np.asarray(x).astype(np.float64)


E2M1 = np.array([0.0, 0.5, 1.0, 1.5, 2.0, 3.0, 4.0, 6.0, -0.0, -0.5, -1.0, -1.5, -2.0, -3.0, -4.0, -6.0])


def pack_weight(w, fmt):
    k, n = w.shape
    w = f64(bf(w)).reshape(k // 32, 32, n)
    amax = np.abs(w).max(1)
    if fmt == "e4m3":
        byte = np.frexp(amax)[1] - 1 + 127 - 7
    else:
        mant, ex = np.frexp(amax / 6.0)
        byte = np.where(mant > 0.5, ex, ex - 1) + 127
    byte = np.clip(np.where(amax > 0, byte, 1), 1, 254)
    scaled = (w * np.exp2(127.0 - byte)[:, None, :]).reshape(k, n).astype(np.float32)
    by_word = np.ascontiguousarray(scaled.reshape(k // 512, 128, 4, n).transpose(0, 1, 3, 2))
    if fmt == "e4m3":
        words = by_word.astype(ml_dtypes.float8_e4m3fn).view(np.uint8)
    else:
        c = by_word.astype(ml_dtypes.float4_e2m1fn).view(np.uint8) & 0xF
        words = c[..., 0::2] | (c[..., 1::2] << 4)
    return np.ascontiguousarray(words), np.ascontiguousarray(byte.astype(np.uint8).reshape(k // 512, 16, n))


def unpack_weight(words, scales, fmt):
    g, p, n, _ = words.shape
    if fmt == "e4m3":
        vals = np.ascontiguousarray(words).view(ml_dtypes.float8_e4m3fn).astype(np.float64)
    else:
        nib = np.empty((g, p, n, 4), np.uint8)
        nib[..., 0::2] = words & 0xF
        nib[..., 1::2] = words >> 4
        vals = E2M1[nib]
    vals = vals * np.repeat(np.exp2(scales.astype(np.float64) - 127.0), 8, axis=1)[..., None]
    return vals.transpose(0, 1, 3, 2).reshape(g * 512, n)
def pack4(w):
    words, scales = pack_weight(w, "e2m1")
    return words.reshape(words.shape[0], 128, -1), scales


def unpack4(words, scales):
    return unpack_weight(words.reshape(words.shape[0], 128, -1, 2), scales, "e2m1")


E4M3FN = np.array([(-1.0 if i & 128 else 1.0) * ((1.0 + (i & 7) / 8.0) * 2.0 ** (((i >> 3) & 15) - 7) if i & 120 else (i & 7) * 2.0 ** -9) for i in range(256)])


def e4m3fn_bytes(y):
    return np.clip(np.asarray(y, np.float64), -448.0, 448.0).astype(np.float32).astype(ml_dtypes.float8_e4m3fn).view(np.uint8)


def e4m3fn_values(b):
    return E4M3FN[b]


T, K, N, B, G = 2048, 1536, 1024, 512, 128


def setup_inputs():
    s, t = mx_kscale(K), mx_kscale(N)
    ent = np.random.standard_normal((T, K)) * s
    ent_scale = (np.abs(ent).reshape(T, K // G, G).max(axis=2) / 448.0).astype(np.float32)
    ent_bytes = e4m3fn_bytes(ent / np.repeat(f64(ent_scale), G, axis=1))
    heads = np.random.standard_normal((N, B)) / np.sqrt(N) / t[:, None]
    heads_words, heads_scales = pack4(heads)
    return {"ent_bytes": ent_bytes,
            "ent_scale": ent_scale,
            "rel": bf(np.random.standard_normal((K, N)) / np.sqrt(K) / s[:, None]),
            "gain": bf((1 + 0.1 * np.random.standard_normal(N)) * t),
            "heads_words": heads_words,
            "heads_scales": heads_scales,
            "prior": bf(0.3 * np.random.standard_normal(T))}


def reference(ent_bytes, ent_scale, rel, gain, heads_words, heads_scales, prior):
    ent = e4m3fn_values(ent_bytes) * np.repeat(f64(ent_scale), G, axis=1)
    z = mxq(ent, 1, "e4m3") @ mxq(f64(rel), 0, "e4m3")
    tails = np.tanh(z) * f64(gain)
    heads = unpack4(heads_words, heads_scales)
    scores = heads.T @ mxq(tails, 1, "e4m3").T
    return scores + f64(prior)

from contextlib import ExitStack

import concourse.mybir as mybir
from concourse.masks import make_identity

T, K, N, B = 2048, 1536, 1024, 512
FLOPS = 2 * T * K * N + 2 * B * N * T

F32 = mybir.dt.float32
BF16 = mybir.dt.bfloat16
I32 = mybir.dt.int32
U32 = mybir.dt.uint32
U8 = mybir.dt.uint8
FP8 = mybir.dt.float8_e4m3fn
FP8X4 = mybir.dt.float8_e4m3fn_x4
FP4X4 = mybir.dt.float4_e2m1fn_x4
ACT = mybir.ActivationFunctionType
ALU = mybir.AluOpType

P = 128
PASS = 4 * P
K_PASSES = K // PASS
N_PASSES = N // PASS
SCALED = 128
CHUNK = 2 * P
CHUNKS = T // CHUNK
LAST = CHUNKS - 1
WIDE = 2 * CHUNK
HEAD_TILES = B // P
EARLY_CHUNKS = 2

TURN_BANKS, Z_BANKS, SCORE_BANKS = 3, 3, 2

FLOW_BUFS, FEW_BUFS = 4, 3
STORE_BUFS = 8

VECTOR_GROUPS = (5, 5, 3, 4, 4, 2, 5, 3)
SCALAR_INTERLEAVES = ((1, 0), (0, 1))


def widens_on_vector(c, i, g):
    return K_PASSES * i + g < VECTOR_GROUPS[c]


def steps(text, chunk=0):
    found = []
    for word in text.split():
        kind, numbers = word.split(":")
        first, *rest = [int(number) for number in numbers.split(".")]
        found.append((kind, chunk + first, *rest))
    return found


def tensor_queue():
    queue = steps(
        "turn:0.0 turn:0.1 turn:0.2 turn:1.0 turn:1.1 turn:1.2 project:0.0.0 project:1.0.0 project:1.0.1 project:0.0.1"
        " turn:2.0 turn:2.1 turn:2.2 project:0.1.0 project:0.1.1 project:1.1.0 project:1.1.1"
    )
    for c in range(EARLY_CHUNKS, CHUNKS):
        w = (c - 3) // 2
        queue += steps("project:0.0.0", c)
        if c < LAST:
            queue += steps("turn:1.0 turn:1.1 turn:1.2", c)
        queue += steps("project:0.0.1", c)
        if 0 <= w and c < LAST:
            queue += steps("score:0.0 score:0.1" if c % 2 else "score:0.3", w)
        queue += steps("project:0.1.0 project:0.1.1", c)
        if c % 2 and c < LAST:
            queue += steps("score:0.2", w)
    return queue + steps("score:2.0 score:2.1 score_end:6.0 score:2.2 score_end:6.1 score:2.3 score_end:7.0 score_end:7.1")


def vector_queue():
    queue = steps(
        "widen:0.0.0 widen:0.1.0 widen:0.1.1 widen:0.0.1 widen:0.0.2 interleave:0.0 quant_rel:0.0"
        " widen:1.0.0 widen:1.1.0 widen:1.1.1 widen:1.0.1 interleave:2.0 widen:1.0.2 quant_rel:1.0"
        " quant_ent:0.0 quant_ent:0.1 quant_rel:2.0 quant_ent:1.0 quant_ent:0.2 interleave:1.1 quant_ent:1.1 quant_ent:1.2"
        " widen:2.0.0 quant_rel:0.1 widen:2.0.1 quant_rel:1.1 interleave:2.1 widen:2.0.2 quant_rel:2.1"
        " widen:3.0.0 widen:3.1.0 gain:0.0 widen:3.0.1 quant_ent:2.0 quant_ent:2.1 quant_ent:2.2 widen:3.0.2"
        " quant_tails:0.0 gain:0.1 gain:1.0 widen:4.0.0 widen:4.1.0 widen:4.0.1 quant_tails:1.0"
        " quant_ent:3.0 quant_ent:3.1 quant_ent:3.2 gain:1.1 widen:4.0.2 gain:2.0 quant_tails:1.1 quant_tails:0.1"
        " widen:5.0.0 quant_tails:2.0 gain:2.1 widen:5.0.1 add:0.0 quant_ent:4.0 quant_ent:4.1 quant_ent:4.2 add:0.1"
    )
    for c in range(3, LAST):
        w = (c - 3) // 2
        slot = steps("gain:0.0 quant_tails:-1.1", c)
        if c % 2 == 0:
            slot += steps("add:0.3", w)
        slot += steps("widen:3.0.0 widen:3.1.0 quant_tails:0.0 gain:0.1 widen:3.0.1", c)
        if c % 2 == 0 and c + 1 < LAST:
            slot += steps("add:1.0", w)
        slot += steps("quant_ent:2.0 quant_ent:2.1 widen:3.1.1 quant_ent:2.2 widen:3.0.2", c)
        if c + 1 < LAST or c % 2:
            slot += steps("add:0.2" if c % 2 else "add:1.1", w)
        for step in slot:
            if step[1] <= LAST and (step[0] != "widen" or widens_on_vector(*step[1:])):
                queue.append(step)
    return queue + steps(
        "gain:7.0 quant_tails:6.1 quant_tails:7.0 add:2.0 gain_end:0 add:2.1 quant_end:0 add_end:6.0 add:2.2"
        " gain_end:1 add_end:6.1 quant_end:1 add_end:7.0 add:2.3 add_end:7.1"
    )


def scalar_queue():
    queue = steps(
        "widen:0.1.2 empty:0.0 empty:0.1 interleave:1.0 widen:1.1.2 empty:0.2 empty:1.0 empty:1.1 interleave:0.1 empty:1.2"
        " widen:2.1.0 tanh:0.0.0 widen:2.1.1 widen:2.1.2 tanh:1.0.0 tanh:1.0.1 tanh:0.0.1 empty:2.0 empty:2.1 empty:2.2"
        " widen:3.1.1 tanh:0.1.0 tanh:0.1.1 tanh:1.1.0 widen:3.1.2 tanh:1.1.1"
    )
    for c in range(EARLY_CHUNKS, CHUNKS):
        slot = steps(
            "tanh:0.0.0 widen:2.1.0 empty:1.0 empty:1.1 empty:1.2 tanh:0.0.1"
            " widen:2.1.1 widen:2.0.2 widen:2.1.2 tanh:0.1.0 tanh:0.1.1",
            c,
        )
        for step in slot:
            if step[1] <= LAST and (step[0] != "widen" or not widens_on_vector(*step[1:])):
                queue.append(step)
    return queue


def producers(step):
    kind, first, *rest = step
    both = range(2)
    if kind == "turn":
        return [("widen", first, i, *rest) for i in both]
    if kind == "project":
        return [("quant_ent", first, g) for g in range(K_PASSES)] + [("quant_rel", g, rest[0]) for g in range(K_PASSES)]
    if kind == "gain":
        return [("tanh", first, *rest, u) for u in both]
    if kind == "gain_end":
        return [("tanh", LAST, 1, u) for u in both]
    if kind == "score":
        return [("quant_tails", 2 * first + d, h) for d in both for h in both]
    if kind == "score_end":
        return [("quant_tails", first, 0), ("quant_end", *rest) if first == LAST else ("quant_tails", first, 1)]
    before = {
        "empty": "turn", "quant_ent": "empty", "quant_rel": "interleave", "tanh": "project",
        "quant_tails": "gain", "quant_end": "gain_end", "add": "score", "add_end": "score_end",
    }
    return [(before[kind], first, *rest)] if kind in before else []


def program_order():
    queues = [tensor_queue(), vector_queue(), scalar_queue()]
    order, written = [], set()
    while any(queues):
        queue = [q for q in queues if q and all(step in written for step in producers(q[0]))][0]
        order.append(queue[0])
        written.add(queue[0])
        queue.remove(queue[0])
    return order


def tile_relation_tail_scores_d4_kernel(tc, ent_bytes, ent_scale, rel, gain, heads_words, heads_scales, prior, out):
    nc = tc.nc
    with ExitStack() as ctx:
        keep = ctx.enter_context(tc.tile_pool(name="keep", bufs=1))
        flow = ctx.enter_context(tc.tile_pool(name="flow", bufs=FLOW_BUFS))
        psum = ctx.enter_context(tc.psum_pool(name="psum", bufs=1))
        ctx.enter_context(tc.manual_schedule())

        identity = keep.tile([P, P], F32, name="identity")
        make_identity(nc, identity[:])

        scale_sb = keep.tile([P, CHUNKS, 2, K // SCALED], F32, name="scale_sb")
        ent_raw = [keep.tile([P, 2, K], U8, name="ent_raw_%d" % c) for c in range(CHUNKS)]
        rel_raw = {}
        for g in range(K_PASSES):
            for h in range(N_PASSES):
                rel_raw[g, h] = keep.tile([P, 4, PASS], BF16, name="rel_raw_%d_%d" % (g, h))
        gain_sb = keep.tile([P, N_PASSES, 4], BF16, name="gain_sb")
        prior_sb = keep.tile([P, T], BF16, name="prior_sb")
        head_words = keep.tile([P, N_PASSES, 2 * B], U8, name="head_words", align_bytes=64)
        head_scales = keep.tile([P, N_PASSES, B], U8, name="head_scales", align_bytes=64)

        def load_scales(chunks):
            rows = ent_scale.rearrange("(c p i) q -> p c (i q)", p=P, i=2)
            nc.sync.dma_start(out=scale_sb[:].rearrange("p c i q -> p c (i q)")[:, chunks, :], in_=rows[:, chunks, :])

        def load_bytes(c, columns):
            rows = ent_bytes[CHUNK * c : CHUNK * (c + 1), :].rearrange("(p i) k -> p i k", i=2)
            nc.sync.dma_start(out=ent_raw[c][:, :, columns], in_=rows[:, :, columns])

        def load_rel(g, h):
            rows = rel[PASS * g : PASS * (g + 1), PASS * h : PASS * (h + 1)]
            nc.sync.dma_start(out=rel_raw[g, h][:], in_=rows.rearrange("(p j) n -> p j n", j=4))

        all_k = slice(0, K)
        load_scales(slice(0, EARLY_CHUNKS))
        for g in range(K_PASSES):
            load_bytes(0, slice(PASS * g, PASS * (g + 1)))
        load_rel(0, 0)
        load_rel(1, 0)
        load_bytes(1, all_k)
        load_rel(2, 0)
        for g in range(K_PASSES):
            load_rel(g, 1)
        load_scales(slice(EARLY_CHUNKS, CHUNKS))
        load_bytes(2, all_k)
        nc.sync.dma_start(out=gain_sb[:], in_=gain.rearrange("(h p t) -> p h t", p=P, t=4))
        load_bytes(3, all_k)
        nc.gpsimd.memset(head_scales[:].bitcast(U32), 0)
        nc.sync.dma_start(out=head_words[:].bitcast(I32), in_=heads_words.rearrange("h p n -> p h n").bitcast(I32))
        for quadrant in range(4):
            rows = heads_scales[:, 4 * quadrant : 4 * quadrant + 4, :].rearrange("h r n -> r h n")
            nc.sync.dma_start(out=head_scales[32 * quadrant : 32 * quadrant + 4, :, :].bitcast(I32), in_=rows.bitcast(I32))
        nc.sync.dma_start(out=prior_sb[:], in_=prior.partition_broadcast(P))
        for c in range(4, CHUNKS):
            load_bytes(c, all_k)

        rel_codes = keep.tile([P, K_PASSES, N], U32, name="rel_codes", align_bytes=64)
        rel_scales = keep.tile([P, K_PASSES, N], U8, name="rel_scales", align_bytes=64)
        made = {}

        def once(key, shape, dtype, bufs=FLOW_BUFS):
            if key not in made:
                made[key] = flow.tile(shape, dtype, name=key[0], bufs=bufs, align_bytes=64)
            return made[key]

        def interleave(g, h):
            grouped = once(("rel_grouped", g, h), [P, 4 * PASS], BF16, bufs=FEW_BUFS)
            target = grouped[:].rearrange("p (t m j) -> p m t j", t=4, j=4)
            source = rel_raw[g, h][:].rearrange("p j (m t) -> p m t j", t=4)
            if (g, h) in SCALAR_INTERLEAVES:
                nc.scalar.copy(out=target, in_=source)
            else:
                nc.vector.tensor_copy(out=target, in_=source)

        def quant_rel(g, h):
            columns = slice(PASS * h, PASS * (h + 1))
            nc.vector.quantize_mx(
                out=rel_codes[:, g, columns].bitcast(FP8X4), scales=rel_scales[:, g, columns], in_=made["rel_grouped", g, h][:]
            )

        def widen(c, i, g):
            values = once(("widened", c), [P, 2, K], BF16)[:, i, PASS * g : PASS * (g + 1)]
            per_pass = PASS // SCALED
            for block in range(per_pass):
                q = per_pass * g + block
                source = ent_raw[c][:, i, SCALED * q : SCALED * (q + 1)].bitcast(FP8)
                scale = scale_sb[:, c, i, q : q + 1]
                if widens_on_vector(c, i, g):
                    target = values.rearrange("p (u m e) -> p m u e", u=2, e=2)[:, 32 * block : 32 * (block + 1), :, :]
                    source = source.rearrange("p (m u e) -> p m u e", u=2, e=2)
                    nc.vector.tensor_scalar(out=target, in0=source, scalar1=scale, scalar2=None, op0=ALU.mult)
                else:
                    target = values[:, SCALED * block : SCALED * (block + 1)]
                    nc.scalar.activation(out=target, in_=source, func=ACT.Copy, scale=scale)

        def turn(c, g):
            turned = psum.tile([P, 4, P], F32, name="turned", bufs=TURN_BANKS)
            made["turned", c, g] = turned
            for i in range(2):
                pairs = made["widened", c][:, i, :].bitcast(F32)[:, 2 * P * g : 2 * P * (g + 1)]
                for u in range(2):
                    chosen = pairs[:, P * u : P * (u + 1)] if widens_on_vector(c, i, g) else pairs[:, u : 2 * P : 2]
                    nc.tensor.transpose(turned[:, 2 * i + u, :], chosen, identity[:])

        def empty(c, g):
            grouped = once(("ent_grouped", c), [P, K_PASSES, 4 * CHUNK], BF16, bufs=FEW_BUFS)
            target = grouped[:, g, :].bitcast(F32).rearrange("p (r s) -> p r s", s=4)
            nc.scalar.copy(out=target, in_=made["turned", c, g][:].rearrange("p s r -> p r s"))

        def quant_ent(c, g):
            codes = once(("ent_codes", c), [P, K_PASSES, CHUNK], U32)
            scales = once(("ent_scales", c), [P, K_PASSES, CHUNK], U8)
            nc.vector.quantize_mx(out=codes[:, g, :].bitcast(FP8X4), scales=scales[:, g, :], in_=made["ent_grouped", c][:, g, :])

        def project(c, h, u):
            z = psum.tile([P, 2, CHUNK], F32, name="z", bufs=Z_BANKS)
            made["z", c, h, u] = z
            for e in range(2):
                first = PASS * h + P * (2 * u + e)
                for g in range(K_PASSES):
                    nc.tensor.matmul_mx(
                        out=z[:, e, :],
                        lhsT=rel_codes[:, g, first : first + P].bitcast(FP8X4),
                        lhsT_scale=rel_scales[:, g, first : first + P],
                        rhs=made["ent_codes", c][:, g, :].bitcast(FP8X4),
                        rhs_scale=made["ent_scales", c][:, g, :],
                        start=(g == 0),
                        stop=(g == K_PASSES - 1),
                    )

        def tanh(c, h, u):
            tanh_z = once(("tanh_z", c, h), [P, 2, CHUNK, 2], F32)
            nc.scalar.activation(out=tanh_z[:, u, :, :], in_=made["z", c, h, u][:].rearrange("p e r -> p r e"), func=ACT.Tanh)

        def times_gain(c, h, first, count):
            tails = once(("tails", c, h), [P, 4 * CHUNK], BF16)
            factor = gain_sb[:, h, :].rearrange("p (u e) -> p u e", u=2).unsqueeze(1).to_broadcast([P, count, 2, 2])
            nc.vector.tensor_tensor(
                out=tails[:, 4 * first : 4 * (first + count)].rearrange("p (r u e) -> p r u e", u=2, e=2),
                in0=made["tanh_z", c, h][:, :, first : first + count, :].rearrange("p u r e -> p r u e"),
                in1=factor,
                op=ALU.mult,
            )

        def quantize_tails(c, h, first, count):
            codes = once(("tail_codes", c // 2), [P, N_PASSES, WIDE], U32, bufs=FEW_BUFS)
            scales = once(("tail_scales", c // 2), [P, N_PASSES, WIDE], U8, bufs=FEW_BUFS)
            columns = slice(CHUNK * (c % 2) + first, CHUNK * (c % 2) + first + count)
            nc.vector.quantize_mx(
                out=codes[:, h, columns].bitcast(FP8X4),
                scales=scales[:, h, columns],
                in_=made["tails", c, h][:, 4 * first : 4 * (first + count)],
            )

        def heads_times_tails(sums, b, w, columns):
            for h in range(N_PASSES):
                nc.tensor.matmul_mx(
                    out=sums,
                    lhsT=head_words[:, h, 2 * P * b : 2 * P * (b + 1)].bitcast(FP4X4),
                    lhsT_scale=head_scales[:, h, P * b : P * (b + 1)],
                    rhs=made["tail_codes", w][:, h, columns].bitcast(FP8X4),
                    rhs_scale=made["tail_scales", w][:, h, columns],
                    start=(h == 0),
                    stop=(h == N_PASSES - 1),
                )

        def score(w, b):
            sums = psum.tile([P, WIDE], F32, name="sums", bufs=SCORE_BANKS)
            made["sums", w, b] = sums
            heads_times_tails(sums[:], b, w, slice(0, WIDE))

        def add(w, b):
            scores = flow.tile([P, WIDE], F32, name="scores", bufs=STORE_BUFS)
            entities = slice(WIDE * w, WIDE * (w + 1))
            nc.vector.tensor_tensor(out=scores[:], in0=made["sums", w, b][:], in1=prior_sb[:, entities], op=ALU.add)
            nc.sync.dma_start(out=out[P * b : P * (b + 1), entities], in_=scores[:])

        def score_end(c, x):
            sums = psum.tile([P, HEAD_TILES, P], F32, name="turned", bufs=TURN_BANKS)
            made["sums_end", c, x] = sums
            first = CHUNK * (c % 2) + P * x
            for b in range(HEAD_TILES):
                heads_times_tails(sums[:, b, :], b, c // 2, slice(first, first + P))

        def add_end(c, x):
            parts = 2 if (c, x) == (LAST, 1) else 1
            count = HEAD_TILES // parts
            entities = slice(CHUNK * c + P * x, CHUNK * c + P * (x + 1))
            for part in range(parts):
                tiles = slice(count * part, count * (part + 1))
                scores = flow.tile([P, count, P], F32, name="scores", bufs=STORE_BUFS)
                nc.vector.tensor_tensor(
                    out=scores[:],
                    in0=made["sums_end", c, x][:, tiles, :],
                    in1=prior_sb[:, entities].unsqueeze(1).to_broadcast([P, count, P]),
                    op=ALU.add,
                )
                nc.sync.dma_start(out=out[:, entities].rearrange("(b p) t -> p b t", p=P)[:, tiles, :], in_=scores[:])

        run = {
            "interleave": interleave,
            "quant_rel": quant_rel,
            "widen": widen,
            "turn": turn,
            "empty": empty,
            "quant_ent": quant_ent,
            "project": project,
            "tanh": tanh,
            "gain": lambda c, h: times_gain(c, h, 0, CHUNK),
            "quant_tails": lambda c, h: quantize_tails(c, h, 0, CHUNK),
            "gain_end": lambda x: times_gain(LAST, 1, P * x, P),
            "quant_end": lambda x: quantize_tails(LAST, 1, P * x, P),
            "score": score,
            "add": add,
            "score_end": score_end,
            "add_end": add_end,
        }
        for kind, *where in program_order():
            run[kind](*where)
